import numpy as np, ml_dtypes
CORES = [1,5,17,21,33,37,49,53]
N = 8
import mx_ref
BF = ml_dtypes.bfloat16
def gentries(a):
    return np.ascontiguousarray(a.reshape(8, 16, -1).transpose(0, 2, 1)).reshape(8, -1)
def gtable(e):
    e = np.asarray(e); return np.ascontiguousarray(e.reshape(8, -1, 16).transpose(0, 2, 1)).reshape(128, -1).astype(np.int32)
def gcols(t, e):
    v = np.concatenate([t.reshape(8, 16, -1, 4), np.zeros((8, 16, 1, 4), BF)], axis=2)
    return np.ascontiguousarray(np.stack([v[g][:, e[g]] for g in range(8)])).reshape(128, -1)
def tile(rs):
    return np.stack(rs, axis=2).reshape(128, -1).astype(BF)
def pick(q, e):
    c = np.concatenate([q[0].reshape(128, -1, 4), np.zeros((128, 1, 4), np.uint8)], axis=1); s = np.concatenate([q[1], np.ones((16, 1), np.uint8)], axis=1)
    return (np.ascontiguousarray(c[:, e].reshape(128, -1)), np.ascontiguousarray(s[:, e]))
def join(*qs):
    return (np.concatenate([q[0] for q in qs], axis=1), np.concatenate([q[1] for q in qs], axis=1))
def put(q, e, v):
    c, s = q[0].reshape(128, -1, 4).copy(), q[1].copy(); c[:, e] = v[0].reshape(128, -1, 4); s[:, e] = v[1]
    return (c.reshape(128, -1), s)
def pk(c, s):
    return (np.ascontiguousarray(c), mx_ref.live(s))
def emit(q):
    return q[0], q[1]
def packed(v, rng):
    q = [mx_ref.quantize(np.ascontiguousarray(v[r])) for r in range(N)]
    return np.stack([a for a, b in q]), np.stack([mx_ref.plane(b, rng) for a, b in q])
def values_of_codes():
    e, c = np.zeros((128, 128, 4), np.float32), np.zeros((128, 2, 4), np.uint8)
    e[np.arange(128), np.arange(128), 0] = 1
    c[:127, :, 0] = np.arange(256).reshape(2, 128).T[:127]
    return mx_ref.matmul(mx_ref.quantize(e.reshape(128, 512).astype(BF)), (c.reshape(128, 8), np.full((16, 2), 127, np.uint8))).T.reshape(-1).astype(np.float64)
CODE_VALUE, SCALE_VALUE = values_of_codes(), 2.0 ** (np.arange(256) - 127.0)
def decode(q):
    return (CODE_VALUE[q[0]].reshape(16, 8, -1, 4) * SCALE_VALUE[q[1]][:, None, :, None] + 0.0).reshape(128, -1).astype(np.float32)
def f(rng, *shape):
    return mx_ref.flush((rng.standard_normal(shape, dtype=np.float32) * np.exp2(rng.integers(-2, 3, shape[:-1] + (1,)))).astype(BF))
def wide(rng, *shape, cols=0):
    v = rng.standard_normal(shape, dtype=np.float32) * np.exp2(rng.integers(-12, 13, shape)).astype(np.float32)
    if cols: v *= np.repeat(np.exp2(rng.integers(-cols, cols + 1, shape[:-2] + (1, shape[-1] // 4))) * (rng.random(shape[:-2] + (1, shape[-1] // 4)) > 0.0625), 4, axis=-1).astype(np.float32)
    return mx_ref.flush(v.astype(BF))
C, H = 320, 160
STEP = [1, 2, 4]
def numbers_of(rng):
    return {"x": np.array(f(rng, N, 128, 4 * C)), "u": np.array(f(rng, N, 128, 512)), "v": np.array(f(rng, N, 128, 512))}
def stored(k):
    return {"nl": np.stack([gtable(k[r]) for r in range(N)])}
def lists(rng):
    return stored(rng.permuted(np.tile(np.arange(C), (N, 8, 1)), axis=2))
def layers(rng, still=()):
    w = np.array(f(rng, N, 128, 2048)).reshape(N, 8, 16, 4, 8, 16, 4)
    for i in still:
        w[:, :, i] = 0
        w[:, :, :, :, :, i] = 0
    return w
def weights(rng, w):
    c, p = packed(np.ascontiguousarray(w).reshape(N, 128, 2048), rng)
    return {"wc": c, "ws": p}
def setup_inputs(rng):
    return {**numbers_of(rng), **lists(rng), **weights(rng, layers(rng))}
def setup_inputs_ties(rng):
    d = numbers_of(rng)
    o = rng.permutation(N)
    k = rng.integers(-1, 2, (N, 8, 3, C)).astype(np.float32)
    k[o[1]] = 1
    x = d["x"].reshape(N, 8, 16, C, 4)
    x[:, :, :3] = 0
    x[:, :, :3, :, 0] = k.astype(BF)
    c = np.ones(N, np.float32)
    c[o[0]] = 0
    c[o[2]] = -1
    u = d["u"].reshape(N, 8, 16, 8, 16, 4)
    u[:, :, :, :, :3] = 0
    g = np.arange(8)
    for j in range(3): u[:, g, j, g, j, 0] = c.astype(BF)[:, None]
    w = layers(rng)
    w[:, :, :, :, :, :8] = 0
    return {"x": x.reshape(N, 128, 4 * C), "u": u.reshape(N, 128, 512), "v": d["v"], **lists(rng), **weights(rng, w)}
def setup_inputs_near(rng):
    d = numbers_of(rng)
    o = rng.permutation(N) % 3
    x = d["x"].astype(np.float32).reshape(N, 8, 16, C, 4)
    u = d["u"].astype(np.float32).reshape(N, 8, 16, 8, 16, 4)
    w = layers(rng, range(8))
    x[:, :, :8] = 0
    u[:, :, :, :, :3] = 0
    g = np.arange(8)
    for r in range(N):
        k, e = (1.0, 1.0) if o[r] == 0 else (2.0 ** -28, 2.0 ** -30)
        if o[r] == 2:
            x[r, :, 8:] = 0
            x[r, :, 8, :, 0] = k
            w[r] = 0
        for j in range(3):
            u[r, g, 6, g, j, 0] = e
            if o[r] < 2:
                s = rng.integers(-1, 2, (8, C)) * k
                x[r, :, 2 * j, :, 0] = 1.125 * s
                x[r, :, 2 * j + 1, :, 0] = -1.25 * s
                u[r, g, 2 * j, g, j, 0] = 1.125 * e
                u[r, g, 2 * j + 1, g, j, 0] = e
            else:
                x[r, :, 9 + j, :, 0] = k * rng.choice([-1.0, 1.0], (8, C))
                u[r, g, 12 + j, g, j, 0] = e
                w[r, g, 9 + j, 0, g, 12 + j, 0] = 2.0 ** -8
        at = [0, C - 1, int(rng.integers(C)), int(rng.integers(C))]
        for h, c in zip(rng.permutation(8)[:4], at): x[r, h, 6, c, 0] = 2.0 ** 30 * rng.choice([-1.0, 1.0])
    return {"x": x.reshape(N, 128, 4 * C).astype(BF), "u": u.reshape(N, 128, 512).astype(BF), "v": d["v"], **lists(rng), **weights(rng, w)}
def setup_inputs_odd(rng):
    d = numbers_of(rng)
    x = (1.0 + (2 * rng.integers(0, 64, (N, 16, 8, C, 4)) + 1) * 2.0 ** -7) * np.exp2(-rng.integers(0, 7, (N, 16, 8, C, 4)).astype(np.float64)) * rng.choice([-1.0, 1.0], (N, 16, 8, C, 4))
    x[:, :, 0, :, 0] = 1.96875 * 2.0 ** 8 * rng.choice([-1.0, 1.0], (N, 16, 1))
    u = d["u"].reshape(N, 16, 8, 128, 4)
    u[:, :, 0] = 0
    return {"x": x.astype(np.float32).reshape(N, 128, 4 * C).astype(BF), "u": u.reshape(N, 128, 512), "v": d["v"], **lists(rng), **weights(rng, layers(rng, (0, 8)))}
def setup_inputs_ends(rng):
    d = numbers_of(rng)
    o, e = rng.permutation(N) % 4, rng.permutation(N) % 4
    x = np.zeros((N, 8, 16, C, 4))
    u = d["u"].astype(np.float32).reshape(N, 8, 16, 8, 16, 4)
    v = d["v"].astype(np.float32)
    w = np.zeros((N, 8, 16, 4, 8, 16, 4), np.float32)
    k = np.tile(np.arange(C), (N, 8, 1))
    def sized(small, low, *q):
        return (1.0 + 0.125 * rng.integers(0, 8, q)) * 2.0 ** -30 if small else (low + 0.1 * rng.random(q)) * 2.0 ** 30
    for r in range(N):
        h = rng.permutation(8)
        c = np.where(h < 2, 0.0, h % 2 * 2.0 - 1.0)[:, None] * np.where((h > 5)[:, None], [1.0, -1.0, 1.0], 1.0)
        c = c[None, None, :, :, None]
        if o[r] == 3:
            x[r] = d["x"][r].astype(np.float32).reshape(8, 16, C, 4)[:, :, :1]
            u[r, :, :, :, :3] *= np.abs(c).astype(np.float32)
        else:
            small = o[r] == 2
            x[r] = sized(small, 0.7, 8, 16, C, 4) * (rng.choice([-1.0, 1.0], (C, 1)) if o[r] == 1 else -1.0)
            u[r, :, :, :, :3] = c * sized(small, 0.9, 8, 16, 8, 3, 4)
            v[r] = sized(small, 0.9, 128, 512) * rng.choice([-1.0, 1.0], (128, 512))
        if o[r] != 2: x[r, :, 14:] = 0
        i, last = np.arange(14), np.arange(14, 16)
        for g in range(8):
            for b in range(4):
                w[r, g, i, b, g, i, b] = 2.0 ** -8 if o[r] == 3 else 2.0
                if o[r] == 2: w[r, g, last, b, g, last, b] = 256.0
        if e[r] == 1: k[r] = C - 1 - np.arange(C)
        if e[r] == 2:
            k[r, :, :H] = 2 * np.arange(H)
            k[r, :, H:] = 2 * np.arange(H)[::-1] + 1
        if e[r] == 3: k[r] = rng.permuted(k[r], axis=1)
    return {"x": x.astype(np.float32).reshape(N, 128, 4 * C).astype(BF), "u": u.reshape(N, 128, 512).astype(BF), "v": v.astype(BF), **stored(k), **weights(rng, w.astype(BF))}
def setup_inputs_spread(rng):
    d = setup_inputs(rng)
    d["x"] = wide(rng, N, 128, 4 * C, cols=6)
    return d
def check_inputs(d):
    b = []
    for k in ("x", "u", "v"):
        a = np.abs(d[k].astype(np.float32))
        if not (np.isfinite(a).all() and ((a == 0) | (a >= 2.0 ** -30) & (a <= 2.0 ** 30)).all()): b.append("a value of " + k)
    none, least, most = [emit(mx_ref.quantize(np.full((128, 16), k, np.float32).astype(BF)))[1][0, 0] for k in (0.0, 2.0 ** -8, 2.0 ** 8)]
    for r in range(N):
        if (np.sort(gentries(d["nl"][r]), axis=1) != np.arange(C)).any(): b.append("nl: a list that is no permutation")
        if ((d["wc"][r] == 0x7F) | (d["wc"][r] == 0xFF)).any(): b.append("wc: a code that is no number")
        s = mx_ref.live(d["ws"][r])
        if ((s != none) & ((s < least) | (s > most))).any(): b.append("ws: a scale out of range")
        if (((d["wc"][r].reshape(16, 8, 512, 4) & 0x7F) != 0) & (s == none)[:, None, :, None]).any(): b.append("wc: a code other than zero under the scale of zeros")
    return b
def ends(n):
    return np.take_along_axis(np.argsort(n, axis=1), n ^ 1, axis=1)
def reference(x, u, v, nl, wc, ws):
    qu = [mx_ref.quantize(u[r]) for r in range(N)]
    lay = [pk(wc[r], ws[r]) for r in range(N)]
    name = [gentries(nl[r]).astype(np.int64) for r in range(N)]
    now = [x[r] for r in range(N)]
    for step in STEP:
        z = []
        for r in range(N):
            s = mx_ref.matmul(qu[r], mx_ref.quantize(now[r])).reshape(8, 16, C)
            for j in range(3):
                d = ends(name[r])
                h = np.where(name[r] % 2 == 0, np.arange(C), d)
                flag = np.take_along_axis(s[:, j], h, axis=1) > 0
                then = np.roll(name[r], -1, axis=0)
                name[r] = np.roll(np.where(flag, np.take_along_axis(then, d, axis=1), then), 1, axis=0)
            z.append(((gcols(now[r], name[r]).astype(np.float32) + gcols(now[r], ends(name[r])).astype(np.float32)) * np.float32(0.5)).astype(BF))
        made = []
        for r in range(N):
            p = (r - step) % N
            m = np.take_along_axis(np.argsort(name[p], axis=1), name[r], axis=1)
            far = gcols(decode(mx_ref.quantize(z[p])).astype(BF), m[:, :H])
            q = mx_ref.quantize(np.ascontiguousarray(np.concatenate([far, gcols(z[r], m[:, H:])], axis=1)))
            made.append(tile([now[r][:, b::4].astype(np.float32) + mx_ref.matmul(pick(lay[r], np.arange(128 * b, 128 * b + 128)), q) * np.float32(0.03125) for b in range(4)]))
        now = made
    y, nm = np.zeros((N, 128, C), np.float32), np.zeros((N, 8, C), np.float32)
    oc, osc = np.zeros((N, 128, 4 * C), np.uint8), np.zeros((N, 16, C), np.uint8)
    for r in range(N):
        q = mx_ref.quantize(now[r])
        y[r] = mx_ref.matmul(mx_ref.quantize(v[r]), q)
        nm[r] = name[r]
        oc[r], osc[r] = emit(q)
    return {"y": y, "nm": nm, "oc": oc, "osc": osc}

@@ -1,0 +1,304 @@
+import numpy as np
+from concourse.bass import DstId, RemoteDMATransfer
+from concourse.mybir import dt, AluOpType as OP, AxisListType, ActivationFunctionType as AF
+
+STEP = [1, 2, 4]
+BF, F32, I32, U16, U8, CODE = "bfloat16", "float32", "int32", "uint16", "uint8", "float8_e4m3fn_x4"
+SCRATCH = {
+    "nli": ("sbuf", [128, 20], I32), "ut": ("sbuf", [128, 512], BF), "vt": ("sbuf", [128, 512], BF),
+    "qu": ("sbuf", [128, 128], CODE), "qus": ("sbuf", [128, 128], U8), "qv": ("sbuf", [128, 128], CODE), "qvs": ("sbuf", [128, 128], U8),
+    "uv": ("sbuf", [128, 384], CODE), "uvs": ("sbuf", [128, 384], U8), "wq": ("sbuf", [128, 512], CODE), "wsp": ("sbuf", [128, 512], U8),
+    "et": ("sbuf", [128, 2048], BF), "eq": ("sbuf", [128, 512], CODE), "es": ("sbuf", [128, 512], U8),
+    "jmp": ("sbuf", [128, 320], I32), "jj": ("sbuf", [128, 320], I32), "jma": ("sbuf", [128, 320], I32), "jja": ("sbuf", [128, 320], I32),
+    "mk": ("sbuf", [128, 320], BF), "rz": ("sbuf", [128, 320], BF), "icf": ("sbuf", [128, 320], BF),
+    "pi": ("sbuf", [128, 20], I32), "pa": ("sbuf", [128, 20], I32), "qi": ("sbuf", [128, 20], I32), "cw": ("sbuf", [128, 20], F32), "ccw": ("sbuf", [128, 20], F32),
+    "ui": ("sbuf", [128, 24], I32), "ua": ("sbuf", [128, 24], I32), "uo": ("sbuf", [128, 24], U16),
+    "fw": ("sbuf", [128, 960], BF), "sg0": ("sbuf", [128, 320], BF), "sg1": ("sbuf", [128, 320], BF), "gf": ("sbuf", [128, 320], BF),
+    "nf0": ("sbuf", [128, 320], BF), "nf1": ("sbuf", [128, 320], BF), "xf0": ("sbuf", [128, 320], BF), "xf1": ("sbuf", [128, 320], BF),
+    "mo0": ("sbuf", [128, 320], BF), "mo1": ("sbuf", [128, 320], BF), "so0": ("sbuf", [128, 320], BF), "so1": ("sbuf", [128, 320], BF),
+    "lst": ("sbuf", [128, 1600], U16), "fs": ("sbuf", [128, 1600], F32), "ist": ("sbuf", [128, 1600], I32),
+    "pub0": ("sbuf", [128, 40], F32), "pub1": ("sbuf", [128, 40], F32), "shl": ("sbuf", [128, 40], F32),
+    "xh": ("sbuf", [128, 1280], BF), "xg": ("sbuf", [128, 1280], BF), "zn": ("sbuf", [128, 1280], BF), "ft": ("sbuf", [128, 640], BF), "vo": ("sbuf", [128, 640], BF), "vf": ("sbuf", [128, 640], BF),
+    "yo": ("sbuf", [128, 320], F32), "nmf": ("sbuf", [128, 320], F32),
+}
+for _k in range(4):
+    SCRATCH.update({"xt%d" % _k: ("sbuf", [128, 1280], BF), "yt%d" % _k: ("sbuf", [128, 1280], BF), "xq%d" % _k: ("sbuf", [128, 320], CODE), "xs%d" % _k: ("sbuf", [128, 320], U8)})
+for _k in range(3):
+    SCRATCH.update({"fq%d" % _k: ("sbuf", [128, 160], CODE), "fp%d" % _k: ("sbuf", [128, 160], U8), "lq%d" % _k: ("sbuf", [128, 160], CODE), "lp%d" % _k: ("sbuf", [128, 160], U8),
+                    "vq%d" % _k: ("sbuf", [128, 320], CODE), "vp%d" % _k: ("sbuf", [128, 320], U8), "ln%d" % _k: ("sbuf", [128, 10], U16), "li%d" % _k: ("sbuf", [128, 20], U16)})
+for _k in range(8):
+    SCRATCH["p%d" % _k] = ("psum", [128, 512], F32)
+QSEM = {"v": "qv_", "a": "qa_", "t": "qt_", "g": "qg_"}
+SEMAPHORES = list(QSEM.values()) + ["d_nl", "d_u", "d_x0", "d_x1", "d_w", "d_v", "d_sh", "d_os", "sent"] + ["r%s%d" % (a, k) for a in "nid" for k in range(3)]
+
+
+def rank_program(g, core, T, topo):
+    rank = T.rank_of(core)
+    if rank is None:
+        return
+    N = len(T.cores)
+    eng = {"v": g.vector, "a": g.scalar, "t": g.tensor, "g": g, "s": g.sync}
+    count, total = {q: 0 for q in QSEM}, {}
+    seen = {q: {} for q in eng}
+    log = {}
+
+    def need(q, reads, writes):
+        own, deps = QSEM.get(q), []
+        for wr, rs in ((False, reads), (True, writes)):
+            for r in rs:
+                ps = SCRATCH.get(r[0], ("x",))[0] == "psum"
+                for (lo, hi, w, sem, val, clk) in log.get(r[0], []):
+                    if not ps and (hi <= r[1] or lo >= r[2]): continue
+                    if not (w or wr or ps): continue
+                    if sem == own and not (w and not wr): continue
+                    deps.append((sem, val, clk))
+        best = {}
+        for sem, val, clk in deps:
+            if val > best.get(sem, (0,))[0]: best[sem] = (val, clk)
+        for sem, (val, clk) in sorted(best.items(), key=lambda e: -len(e[1][1])):
+            if seen[q].get(sem, 0) >= val: continue
+            eng[q].wait_ge(T.sem[sem], val)
+            for s, v in list(clk.items()) + [(sem, val)]:
+                if seen[q].get(s, 0) < v: seen[q][s] = v
+
+    def note(accesses, w, sem, val, clk):
+        for r in accesses:
+            a = log.setdefault(r[0], [])
+            if w and r[3] == 1: a[:] = [e for e in a if not (r[1] <= e[0] and e[1] <= r[2])]
+            a.append((r[1], r[2], w, sem, val, clk))
+
+    def op(q, fn, writes, reads):
+        need(q, reads, writes)
+        count[q] += 1
+        fn().then_inc(T.sem[QSEM[q]], 1)
+        clk = dict(seen[q])
+        clk[QSEM[q]] = count[q]
+        note(reads, False, QSEM[q], count[q], clk)
+        note(writes, True, QSEM[q], count[q], clk)
+
+    def dma(sem, moves):
+        for q, fn, writes, reads in moves: need(q, reads, writes)
+        clk = {}
+        for q, fn, writes, reads in moves:
+            fn(eng[q]).then_inc(T.sem[sem], 16)
+            total[sem] = total.get(sem, 0) + 16
+            for s, v in seen[q].items(): clk[s] = max(v, clk.get(s, 0))
+        for q, fn, writes, reads in moves:
+            note(reads, False, sem, total[sem], clk)
+        for q, fn, writes, reads in moves:
+            note([(r[0], r[1], r[2], 2) for r in writes], True, sem, total[sem], clk)
+
+    def arrives(sem, val, regions):
+        total[sem] = val
+        note(regions, True, sem, val, {})
+
+    def send(dst, out, inn, sem, region):
+        need("g", [region], [])
+        rid, pid, _ = topo.addr(dst)
+        es = topo.engines(core, dst)[:8]
+        g.remote_dma(out, inn, T.sem[sem], T.sem["sent"], pid, rid, sum(1 << e for e in es))
+        total["sent"] = total.get("sent", 0) + len(es)
+
+    ENG = 8
+
+    def R(name, lo=0, hi=None, st=1): return (name, lo, SCRATCH[name][1][1] if hi is None else hi, st)
+    def ap(r): return T[r[0]][:, r[1]:r[2]:r[3]] if r[3] != 1 else T[r[0]][:, r[1]:r[2]]
+    slots = {"lst": 0, "fs": 0, "ist": 0}
+    def new(name, n=20):
+        a = slots[name]
+        slots[name] += n
+        return R(name, a, a + n)
+    def part(r, a, b): return (r[0], r[1] + a, r[1] + b, 1)
+
+    def tt(out, a, b, o): op("v", lambda: g.vector.tensor_tensor(ap(out), ap(a), ap(b), o), [out], [a, b])
+    def ts(out, a, s1, o1, s2=None, o2=None):
+        if o2 is None: op("v", lambda: g.vector.tensor_scalar(ap(out), ap(a), s1, None, o1), [out], [a])
+        else: op("v", lambda: g.vector.tensor_scalar(ap(out), ap(a), s1, s2, o1, o2), [out], [a])
+    def cp(out, a): op("v", lambda: g.vector.tensor_copy(ap(out), ap(a)), [out], [a])
+    def gv(out, win, off): op("v", lambda: g.vector.tensor_copy(ap(out), ap(win).indirect(ap(off))), [out], [win, off])
+    def ga(out, win, off): op("a", lambda: g.scalar.activation(ap(out), ap(win).indirect(ap(off)), AF.Copy), [out], [win, off])
+    def gt(out, win, off, b, o): op("v", lambda: g.vector.tensor_tensor(ap(out), ap(win).indirect(ap(off)), ap(b), o), [out], [win, off, b])
+    def act(out, a, scale=1.0): op("a", lambda: g.scalar.activation(ap(out), ap(a), AF.Copy, scale=scale), [out], [a])
+    def quant(q, s, a): op("v", lambda: g.vector.quantize_mx(ap(q), ap(s), ap(a)), [q, s], [a])
+    def mm(out, l, ls, r, rs): op("t", lambda: g.tensor.matmul_mx(ap(out), ap(l), ap(ls), ap(r), ap(rs), True, True), [out], [l, ls, r, rs])
+    def iota(out, pattern, base, cm, flag=False):
+        op("g", lambda: g.iota(ap(out), pattern, base, cm, allow_small_or_imprecise_dtypes=True) if flag else g.iota(ap(out), pattern, base, cm), [out], [])
+    turn = [0]
+    def scan(n):
+        m, s = R("mo%d" % turn[0], 0, n), R("so%d" % turn[0], 0, n)
+        op("v", lambda: g.vector.tensor_tensor_scan(ap(s), T["rz"][:, 0:n], ap(m), 0.0, OP.mult, OP.add), [s], [m, R("rz", 0, n)])
+        turn[0] ^= 1
+        return (s[0], 15, n, 16)
+    def pick(win, off, n=320):
+        gt(R("mo%d" % turn[0], 0, n), win, off, R("mk", 0, n), OP.mult)
+        return scan(n)
+    def wrapped(v, n=20):
+        o = new("lst", n)
+        ts(o, v, 160.0, OP.add)
+        return o
+
+    dma("d_nl", [("s", lambda e: e.dma_start(T.nli[:], T.nl[:]), [R("nli")], [])])
+    dma("d_u", [("a", lambda e: e.dma_start(T.ut[:], T.u[:]), [R("ut")], [])])
+    for h, q in ((0, "s"), (1, "a")):
+        dma("d_x%d" % h, [(q, lambda e, h=h: e.dma_start(T.xt0[:, 640 * h:640 * h + 640], T.x[:, 640 * h:640 * h + 640]), [R("xt0", 640 * h, 640 * h + 640)], [])])
+    dma("d_w", [("s", lambda e: e.dma_start(T.wq[:, 0:512].bitcast(dt.uint8), T.wc[:, 0:2048]), [R("wq")], []),
+                ("s", lambda e: e.dma_start(T.wsp[:, 0:512], T.ws[:, 0:512]), [R("wsp")], [])])
+    dma("d_v", [("s", lambda e: e.dma_start(T.vt[:], T.v[:]), [R("vt")], [])])
+
+    iota(R("pi"), [[0, 20]], 0, 1)
+    iota(R("qi"), [[16, 20]], 0, 0)
+    iota(R("ui"), [[1, 3], [16, 8]], -16, 0)
+    iota(R("icf"), [[1, 320]], -160, 0, True)
+    iota(R("jmp"), [[1, 320]], 128, -1)
+    iota(R("jj"), [[1, 320]], 0, 0)
+    op("v", lambda: g.vector.memset(T.et[:], 1.0), [R("et")], [])
+    ts(R("pa"), R("pi"), 15, OP.bitwise_and)
+    tt(R("cw"), R("pa"), R("qi"), OP.add)
+    ts(R("ccw"), R("cw"), -160.0, OP.add)
+    ts(R("ua"), R("ui"), 127, OP.bitwise_and)
+    cp(R("uo"), R("ua"))
+    nI = R("nli")
+    nW, par = new("lst"), new("ist")
+    cp(nW, nI)
+    ts(par, nI, 1, OP.bitwise_and)
+    def other(nI, par):
+        a, b, o = new("ist"), new("ist"), new("lst")
+        ts(a, par, -2.0, OP.mult, 1.0, OP.add)
+        tt(b, nI, a, OP.add)
+        cp(o, b)
+        return o
+    nxW = other(nI, par)
+    NF, XF, SG = [R("nf0"), R("nf1")], [R("xf0"), R("xf1")], [R("sg0"), R("sg1")]
+    ga(NF[0], R("icf"), nW)
+    op("v", lambda: g.vector.tensor_copy(ap(XF[0]).indirect(ap(nxW)), ap(R("icf"))), [XF[0]], [nxW, R("icf")])
+    ts(R("jma"), R("jmp"), 15, OP.bitwise_and)
+    ts(R("mk"), R("jma"), 0.0, OP.is_equal)
+    ts(R("jja"), R("jj"), 15, OP.bitwise_and)
+    ts(R("rz"), R("jja"), 0.0, OP.is_gt)
+    at = [0]
+    def publish(xf, nW, par):
+        pub, c = "pub%d" % at[0], R("cw")
+        at[0] ^= 1
+        v = pick(xf, nW)
+        dmc, h, t = R(pub, 0, 20), R(pub, 20, 40), new("fs")
+        tt(dmc, v, R("ccw"), OP.subtract)
+        tt(t, par, dmc, OP.mult)
+        tt(h, t, c, OP.add)
+        dma("d_sh", [("s", lambda e: e.dma_start(T.shl[16:128, :], T[pub][0:112, :]), [R("shl")], [R(pub)]),
+                     ("s", lambda e: e.dma_start(T.shl[0:16, :], T[pub][112:128, :]), [R("shl")], [R(pub)])])
+    publish(XF[0], nW, par)
+    tt(R("mo%d" % turn[0]), XF[0], R("mk"), OP.mult)
+    ixW = wrapped(scan(320))
+    quant(R("qu"), R("qus"), R("ut"))
+    op("v", lambda: g.vector.tensor_copy(T.uv[:, 0:384].bitcast(dt.uint32), T.qu[:, 0:128].bitcast(dt.uint32).indirect(T.uo[:, 0:24])), [R("uv")], [R("qu"), R("uo")])
+    op("a", lambda: g.scalar.activation(T.uvs[:, 0:384], T.qus[:, 0:128].indirect(T.uo[:, 0:24]), AF.Copy), [R("uvs")], [R("qus"), R("uo")])
+
+    def bank(half, b): return R("p%d" % (4 * half + b), 0, 160)
+    def scores(k, half):
+        c = 160 * half
+        q, s = R("xq%d" % k, c, c + 160), R("xs%d" % k, c, c + 160)
+        quant(q, s, R("xt%d" % k, 4 * c, 4 * c + 640))
+        if k < 3:
+            for j in range(3):
+                mm(bank(half, j), R("uv", 128 * j, 128 * j + 128), R("uvs", 128 * j, 128 * j + 128), q, s)
+    def flags(half, j):
+        ts(R("fw", 320 * j + 160 * half, 320 * j + 160 * half + 160), bank(half, j), 0.0, OP.is_gt)
+    def halves(k):
+        act(R("xg"), R("xt%d" % k), 0.5)
+        for b in range(4): act(R("xh", 320 * b, 320 * b + 320), (("xt%d" % k), b, 1280, 4), 0.5)
+
+    scores(0, 0)
+    scores(0, 1)
+    for h in (0, 1): flags(h, 0)
+    cur = [0]
+    for k, s in enumerate(STEP):
+        src, dst = T.cores[(rank - s) % N], T.cores[(rank + s) % N]
+        rn, ri, rd = "rn%d" % k, "ri%d" % k, "rd%d" % k
+        for j in range(3):
+            last = j == 2
+            nf, xf, sg = NF[cur[0]], XF[cur[0]], SG[cur[0]]
+            cur[0] ^= 1
+            nf2, xf2 = NF[cur[0]], XF[cur[0]]
+            h, t, u, sW = new("lst"), new("fs"), new("fs"), new("lst")
+            cp(h, R("shl", 20, 40))
+            v = pick(R("fw", 320 * j, 320 * j + 320), h)
+            tt(t, v, R("shl", 0, 20), OP.mult)
+            tt(u, t, R("cw"), OP.add)
+            cp(sW, u)
+            ga(sg, R("icf"), sW)
+            ga(xf2, sg, ixW)
+            v = pick(nf, sW)
+            nW = wrapped(v)
+            if last: send(src, T["ln%d" % k][:, 0:10], ap(part(nW, 0, 10)), rn, part(nW, 0, 10))
+            if not last:
+                nI, par = new("ist"), new("ist")
+                ts(nI, v, 160.0, OP.add)
+                ts(par, nI, 1, OP.bitwise_and)
+                publish(xf2, nW, par)
+                ixW = wrapped(pick(sg, ixW))
+                if j == 0:
+                    for jj in (1, 2):
+                        for hh in (0, 1): flags(hh, jj)
+                    halves(k)
+                    if k == 0:
+                        ts(R("yt0"), R("xt0"), 32.0, OP.mult)
+                        op("g", lambda: g.affine_select(T.et[:, 0:512], T.et[:, 0:512], [[1, 512]], OP.is_equal, 0.0, 0, -4), [R("et", 0, 512)], [R("et", 0, 512)])
+                        for b in range(1, 4):
+                            op("g", lambda b=b: g.affine_select(T.et[:, 512 * b:512 * b + 512], T.et[:, 512 * b:512 * b + 512], [[1, 512]], OP.is_equal, 0.0, -b, -4), [R("et", 512 * b, 512 * b + 512)], [R("et", 512 * b, 512 * b + 512)])
+                if j == 1 and k == 0: quant(R("eq"), R("es"), R("et"))
+                ga(nf2, nf, sW)
+            else:
+                nI, par = new("ist"), new("ist")
+                ixW = wrapped(pick(sg, ixW))
+                send(dst, T["li%d" % k][:, 0:20], ap(ixW), ri, ixW)
+                ga(nf2, nf, sW)
+                ts(nI, v, 160.0, OP.add)
+        for b in range(4):
+            w = R("xh", 320 * b, 320 * b + 320)
+            gt(R("zn", 320 * b, 320 * b + 320), w, ixW, ("xg", b, 1280, 4), OP.add)
+        arrives(rn, ENG, [R("ln%d" % k)])
+        for b in range(4):
+            (gv if b < 2 else ga)(("ft", b, 640, 4), R("zn", 320 * b, 320 * b + 320), R("ln%d" % k))
+        fq, fp = R("fq%d" % k), R("fp%d" % k)
+        quant(fq, fp, R("ft"))
+        send(dst, T["lq%d" % k][:, 0:160].bitcast(dt.uint8), ap(fq).bitcast(dt.uint8), rd, fq)
+        send(dst, T["lp%d" % k][:, 0:160], ap(fp), rd, fp)
+        ts(par, nI, 1, OP.bitwise_and)
+        nxW = other(nI, par)
+        arrives(ri, ENG, [R("li%d" % k)])
+        ga(R("gf"), nf2, R("li%d" % k))
+        if k < 2: publish(xf2, nW, par)
+        kW = wrapped(pick(R("gf"), part(nxW, 10, 20), 160), 10)
+        for b in range(4):
+            (gv if b < 2 else ga)(("vo", b, 640, 4), R("zn", 320 * b, 320 * b + 320), kW)
+        def layer(half, tile):
+            c = 160 * half
+            q, p = R("vq%d" % k, c, c + 160), R("vp%d" % k, c, c + 160)
+            quant(q, p, R(tile))
+            for b in range(4): mm(bank(half, b), R("wq", 128 * b, 128 * b + 128), R("wsp", 128 * b, 128 * b + 128), q, p)
+            for b in range(4): tt(("yt%d" % (k + 1), 4 * c + b, 4 * c + 640, 4), bank(half, b), ("yt%d" % k, 4 * c + b, 4 * c + 640, 4), OP.add)
+            ts(R("xt%d" % (k + 1), 4 * c, 4 * c + 640), R("yt%d" % (k + 1), 4 * c, 4 * c + 640), 0.03125, OP.mult)
+            scores(k + 1, half)
+            if k < 2:
+                for jj in ((0, 1, 2) if half else (0,)): flags(half, jj)
+            else: out(half)
+        def out(half):
+            c = 160 * half
+            q, p = R("xq3", c, c + 160), R("xs3", c, c + 160)
+            mm(bank(half, 0), R("qv"), R("qvs"), q, p)
+            dma("d_os", [("s", lambda e: e.dma_start(T.oc[:, 4 * c:4 * c + 640], ap(q).bitcast(dt.uint8)), [], [q])] +
+                [("s", lambda e, i=i: e.dma_start(T.osc[4 * i:4 * i + 4, c:c + 160], T.xs3[32 * i:32 * i + 4, c:c + 160]), [], [p]) for i in range(4)])
+            y = R("yo", c, c + 160)
+            act(y, bank(half, 0))
+            dma("d_os", [("a", lambda e: e.dma_start(T.y[:, c:c + 160], ap(y)), [], [y])])
+        if k == 2:
+            quant(R("qv"), R("qvs"), R("vt"))
+            ts(R("nmf"), nf2, 160.0, OP.add)
+            dma("d_os", [("s", lambda e: e.dma_start(T.nm[:], T.nmf[0:128:16, :]), [], [R("nmf")])])
+        layer(1, "vo")
+        arrives(rd, 2 * ENG, [R("lq%d" % k), R("lp%d" % k)])
+        for b in range(4): mm(bank(0, b), R("eq", 128 * b, 128 * b + 128), R("es", 128 * b, 128 * b + 128), R("lq%d" % k), R("lp%d" % k))
+        for b in (0, 2, 1, 3): (cp if b % 2 else act)(("vf", b, 640, 4), bank(0, b))
+        layer(0, "vf")
+    for q, sem in QSEM.items(): total[sem] = count[q]
+    for sem, val in total.items(): g.wait_ge(T.sem[sem], val)

@@ -9,7 +9,7 @@ SCRATCH = {
     "qu": ("sbuf", [128, 128], CODE), "qus": ("sbuf", [128, 128], U8), "qv": ("sbuf", [128, 128], CODE), "qvs": ("sbuf", [128, 128], U8),
     "uv": ("sbuf", [128, 384], CODE), "uvs": ("sbuf", [128, 384], U8), "wq": ("sbuf", [128, 512], CODE), "wsp": ("sbuf", [128, 512], U8),
     "et": ("sbuf", [128, 2048], BF), "eq": ("sbuf", [128, 512], CODE), "es": ("sbuf", [128, 512], U8),
-    "jmp": ("sbuf", [128, 320], I32), "jj": ("sbuf", [128, 320], I32), "jma": ("sbuf", [128, 320], I32), "jja": ("sbuf", [128, 320], I32),
+    "jmp": ("sbuf", [128, 16], I32), "jma": ("sbuf", [128, 16], I32),
     "mk": ("sbuf", [128, 320], BF), "rz": ("sbuf", [128, 320], BF), "icf": ("sbuf", [128, 320], BF),
     "pi": ("sbuf", [128, 20], I32), "pa": ("sbuf", [128, 20], I32), "qi": ("sbuf", [128, 20], I32), "cw": ("sbuf", [128, 20], F32), "ccw": ("sbuf", [128, 20], F32),
     "ui": ("sbuf", [128, 24], I32), "ua": ("sbuf", [128, 24], I32), "uo": ("sbuf", [128, 24], U16),
@@ -47,10 +47,11 @@ def rank_program(g, core, T, topo):
         for wr, rs in ((False, reads), (True, writes)):
             for r in rs:
                 ps = SCRATCH.get(r[0], ("x",))[0] == "psum"
-                for (lo, hi, w, sem, val, clk) in log.get(r[0], []):
+                for (lo, hi, w, sem, val, clk, st) in log.get(r[0], []):
                     if not ps and (hi <= r[1] or lo >= r[2]): continue
+                    if not ps and st == r[3] > 2 and (lo - r[1]) % st: continue
                     if not (w or wr or ps): continue
-                    if sem == own and not (w and not wr): continue
+                    if sem == own and not w: continue
                     deps.append((sem, val, clk))
         best = {}
         for sem, val, clk in deps:
@@ -65,7 +66,7 @@ def rank_program(g, core, T, topo):
         for r in accesses:
             a = log.setdefault(r[0], [])
             if w and r[3] == 1: a[:] = [e for e in a if not (r[1] <= e[0] and e[1] <= r[2])]
-            a.append((r[1], r[2], w, sem, val, clk))
+            a.append((r[1], r[2], w, sem, val, clk, r[3]))
 
     def op(q, fn, writes, reads):
         need(q, reads, writes)
@@ -148,15 +149,18 @@ def rank_program(g, core, T, topo):
     iota(R("pi"), [[0, 20]], 0, 1)
     iota(R("qi"), [[16, 20]], 0, 0)
     iota(R("ui"), [[1, 3], [16, 8]], -16, 0)
+    iota(R("jmp"), [[1, 16]], 128, -1)
     iota(R("icf"), [[1, 320]], -160, 0, True)
-    iota(R("jmp"), [[1, 320]], 128, -1)
-    iota(R("jj"), [[1, 320]], 0, 0)
-    op("v", lambda: g.vector.memset(T.et[:], 1.0), [R("et")], [])
+    op("v", lambda: g.vector.memset(T.rz[:], 1.0), [R("rz")], [])
+    op("v", lambda: g.vector.memset(T.rz[:, 0:320:16], 0.0), [("rz", 0, 320, 16)], [])
     ts(R("pa"), R("pi"), 15, OP.bitwise_and)
     tt(R("cw"), R("pa"), R("qi"), OP.add)
     ts(R("ccw"), R("cw"), -160.0, OP.add)
     ts(R("ua"), R("ui"), 127, OP.bitwise_and)
     cp(R("uo"), R("ua"))
+    ts(R("jma"), R("jmp"), 15, OP.bitwise_and)
+    ts(R("mk", 0, 16), R("jma"), 0.0, OP.is_equal)
+    for a, b in ((16, 32), (32, 64), (64, 128), (128, 256), (256, 320)): cp(R("mk", a, b), R("mk", 0, b - a))
     nI = R("nli")
     nW, par = new("lst"), new("ist")
     cp(nW, nI)
@@ -171,10 +175,6 @@ def rank_program(g, core, T, topo):
     NF, XF, SG = [R("nf0"), R("nf1")], [R("xf0"), R("xf1")], [R("sg0"), R("sg1")]
     ga(NF[0], R("icf"), nW)
     op("v", lambda: g.vector.tensor_copy(ap(XF[0]).indirect(ap(nxW)), ap(R("icf"))), [XF[0]], [nxW, R("icf")])
-    ts(R("jma"), R("jmp"), 15, OP.bitwise_and)
-    ts(R("mk"), R("jma"), 0.0, OP.is_equal)
-    ts(R("jja"), R("jj"), 15, OP.bitwise_and)
-    ts(R("rz"), R("jja"), 0.0, OP.is_gt)
     at = [0]
     def publish(xf, nW, par):
         pub, c = "pub%d" % at[0], R("cw")
@@ -187,8 +187,6 @@ def rank_program(g, core, T, topo):
         dma("d_sh", [("s", lambda e: e.dma_start(T.shl[16:128, :], T[pub][0:112, :]), [R("shl")], [R(pub)]),
                      ("s", lambda e: e.dma_start(T.shl[0:16, :], T[pub][112:128, :]), [R("shl")], [R(pub)])])
     publish(XF[0], nW, par)
-    tt(R("mo%d" % turn[0]), XF[0], R("mk"), OP.mult)
-    ixW = wrapped(scan(320))
     quant(R("qu"), R("qus"), R("ut"))
     op("v", lambda: g.vector.tensor_copy(T.uv[:, 0:384].bitcast(dt.uint32), T.qu[:, 0:128].bitcast(dt.uint32).indirect(T.uo[:, 0:24])), [R("uv")], [R("qu"), R("uo")])
     op("a", lambda: g.scalar.activation(T.uvs[:, 0:384], T.qus[:, 0:128].indirect(T.uo[:, 0:24]), AF.Copy), [R("uvs")], [R("qus"), R("uo")])
@@ -201,6 +199,10 @@ def rank_program(g, core, T, topo):
         if k < 3:
             for j in range(3):
                 mm(bank(half, j), R("uv", 128 * j, 128 * j + 128), R("uvs", 128 * j, 128 * j + 128), q, s)
+    def signs(half, j):
+        f = R("fw", 320 * j + 160 * half, 320 * j + 160 * half + 160)
+        op("a", lambda: g.scalar.activation(ap(f), ap(bank(half, j)), AF.Sign), [f], [bank(half, j)])
+        op("a", lambda: g.scalar.activation(ap(f), ap(f), AF.Relu), [f], [f])
     def flags(half, j):
         ts(R("fw", 320 * j + 160 * half, 320 * j + 160 * half + 160), bank(half, j), 0.0, OP.is_gt)
     def halves(k):
@@ -209,6 +211,8 @@ def rank_program(g, core, T, topo):
 
     scores(0, 0)
     scores(0, 1)
+    tt(R("mo%d" % turn[0]), XF[0], R("mk"), OP.mult)
+    ixW = wrapped(scan(320))
     for h in (0, 1): flags(h, 0)
     cur = [0]
     for k, s in enumerate(STEP):
@@ -227,6 +231,8 @@ def rank_program(g, core, T, topo):
             cp(sW, u)
             ga(sg, R("icf"), sW)
             ga(xf2, sg, ixW)
+            if j == 0:
+                for hh, jj in ((0, 1), (0, 2)) if k else ((0, 1), (1, 1), (0, 2), (1, 2)): signs(hh, jj)
             v = pick(nf, sW)
             nW = wrapped(v)
             if last: send(src, T["ln%d" % k][:, 0:10], ap(part(nW, 0, 10)), rn, part(nW, 0, 10))
@@ -237,10 +243,9 @@ def rank_program(g, core, T, topo):
                 publish(xf2, nW, par)
                 ixW = wrapped(pick(sg, ixW))
                 if j == 0:
-                    for jj in (1, 2):
-                        for hh in (0, 1): flags(hh, jj)
                     halves(k)
                     if k == 0:
+                        op("v", lambda: g.vector.memset(T.et[:], 1.0), [R("et")], [])
                         ts(R("yt0"), R("xt0"), 32.0, OP.mult)
                         op("g", lambda: g.affine_select(T.et[:, 0:512], T.et[:, 0:512], [[1, 512]], OP.is_equal, 0.0, 0, -4), [R("et", 0, 512)], [R("et", 0, 512)])
                         for b in range(1, 4):
@@ -267,10 +272,10 @@ def rank_program(g, core, T, topo):
         nxW = other(nI, par)
         arrives(ri, ENG, [R("li%d" % k)])
         ga(R("gf"), nf2, R("li%d" % k))
-        if k < 2: publish(xf2, nW, par)
         kW = wrapped(pick(R("gf"), part(nxW, 10, 20), 160), 10)
         for b in range(4):
-            (gv if b < 2 else ga)(("vo", b, 640, 4), R("zn", 320 * b, 320 * b + 320), kW)
+            ga(("vo", b, 640, 4), R("zn", 320 * b, 320 * b + 320), kW)
+        if k < 2: publish(xf2, nW, par)
         def layer(half, tile):
             c = 160 * half
             q, p = R("vq%d" % k, c, c + 160), R("vp%d" % k, c, c + 160)
@@ -280,7 +285,7 @@ def rank_program(g, core, T, topo):
             ts(R("xt%d" % (k + 1), 4 * c, 4 * c + 640), R("yt%d" % (k + 1), 4 * c, 4 * c + 640), 0.03125, OP.mult)
             scores(k + 1, half)
             if k < 2:
-                for jj in ((0, 1, 2) if half else (0,)): flags(half, jj)
+                flags(half, 0)
             else: out(half)
         def out(half):
             c = 160 * half
@@ -299,6 +304,8 @@ def rank_program(g, core, T, topo):
         arrives(rd, 2 * ENG, [R("lq%d" % k), R("lp%d" % k)])
         for b in range(4): mm(bank(0, b), R("eq", 128 * b, 128 * b + 128), R("es", 128 * b, 128 * b + 128), R("lq%d" % k), R("lp%d" % k))
         for b in (0, 2, 1, 3): (cp if b % 2 else act)(("vf", b, 640, 4), bank(0, b))
+        if k < 2:
+            for jj in (1, 2): signs(1, jj)
         layer(0, "vf")
     for q, sem in QSEM.items(): total[sem] = count[q]
     for sem, val in total.items(): g.wait_ge(T.sem[sem], val)

import numpy as np
from concourse.bass import DstId, RemoteDMATransfer
from concourse.mybir import dt, AluOpType as OP, AxisListType, ActivationFunctionType as AF

STEP = [1, 2, 4]
BF, F32, I32, U16, U8, CODE = "bfloat16", "float32", "int32", "uint16", "uint8", "float8_e4m3fn_x4"
SCRATCH = {
    "nli": ("sbuf", [128, 20], I32), "ut": ("sbuf", [128, 512], BF), "vt": ("sbuf", [128, 512], BF),
    "qu": ("sbuf", [128, 128], CODE), "qus": ("sbuf", [128, 128], U8), "qv": ("sbuf", [128, 128], CODE), "qvs": ("sbuf", [128, 128], U8),
    "uv": ("sbuf", [128, 384], CODE), "uvs": ("sbuf", [128, 384], U8), "wq": ("sbuf", [128, 512], CODE), "wsp": ("sbuf", [128, 512], U8),
    "et": ("sbuf", [128, 2048], BF), "eq": ("sbuf", [128, 512], CODE), "es": ("sbuf", [128, 512], U8),
    "jmp": ("sbuf", [128, 16], I32), "jma": ("sbuf", [128, 16], I32),
    "mk": ("sbuf", [128, 320], BF), "rz": ("sbuf", [128, 320], BF), "icf": ("sbuf", [128, 320], BF),
    "pi": ("sbuf", [128, 20], I32), "pa": ("sbuf", [128, 20], I32), "qi": ("sbuf", [128, 20], I32), "cw": ("sbuf", [128, 20], F32), "ccw": ("sbuf", [128, 20], F32),
    "ui": ("sbuf", [128, 24], I32), "ua": ("sbuf", [128, 24], I32), "uo": ("sbuf", [128, 24], U16),
    "fw": ("sbuf", [128, 960], BF), "sg0": ("sbuf", [128, 320], BF), "sg1": ("sbuf", [128, 320], BF), "gf": ("sbuf", [128, 320], BF),
    "nf0": ("sbuf", [128, 320], BF), "nf1": ("sbuf", [128, 320], BF), "xf0": ("sbuf", [128, 320], BF), "xf1": ("sbuf", [128, 320], BF),
    "mo0": ("sbuf", [128, 320], BF), "mo1": ("sbuf", [128, 320], BF), "so0": ("sbuf", [128, 320], BF), "so1": ("sbuf", [128, 320], BF),
    "lst": ("sbuf", [128, 1600], U16), "fs": ("sbuf", [128, 1600], F32), "ist": ("sbuf", [128, 1600], I32),
    "pub0": ("sbuf", [128, 40], F32), "pub1": ("sbuf", [128, 40], F32), "shl": ("sbuf", [128, 40], F32),
    "xh": ("sbuf", [128, 1280], BF), "xg": ("sbuf", [128, 1280], BF), "zn": ("sbuf", [128, 1280], BF), "ft": ("sbuf", [128, 640], BF), "vo": ("sbuf", [128, 640], BF), "vf": ("sbuf", [128, 640], BF),
    "yo": ("sbuf", [128, 320], F32), "nmf": ("sbuf", [128, 320], F32),
}
for _k in range(4):
    SCRATCH.update({"xt%d" % _k: ("sbuf", [128, 1280], BF), "yt%d" % _k: ("sbuf", [128, 1280], BF), "xq%d" % _k: ("sbuf", [128, 320], CODE), "xs%d" % _k: ("sbuf", [128, 320], U8)})
for _k in range(3):
    SCRATCH.update({"fq%d" % _k: ("sbuf", [128, 160], CODE), "fp%d" % _k: ("sbuf", [128, 160], U8), "lq%d" % _k: ("sbuf", [128, 160], CODE), "lp%d" % _k: ("sbuf", [128, 160], U8),
                    "vq%d" % _k: ("sbuf", [128, 320], CODE), "vp%d" % _k: ("sbuf", [128, 320], U8), "ln%d" % _k: ("sbuf", [128, 10], U16), "li%d" % _k: ("sbuf", [128, 20], U16)})
for _k in range(8):
    SCRATCH["p%d" % _k] = ("psum", [128, 512], F32)
QSEM = {"v": "qv_", "a": "qa_", "t": "qt_", "g": "qg_"}
SEMAPHORES = list(QSEM.values()) + ["d_nl", "d_u", "d_x0", "d_x1", "d_w", "d_v", "d_sh", "d_os", "sent"] + ["r%s%d" % (a, k) for a in "nid" for k in range(3)]


def rank_program(g, core, T, topo):
    rank = T.rank_of(core)
    if rank is None:
        return
    N = len(T.cores)
    eng = {"v": g.vector, "a": g.scalar, "t": g.tensor, "g": g, "s": g.sync}
    count, total = {q: 0 for q in QSEM}, {}
    seen = {q: {} for q in eng}
    log = {}

    def need(q, reads, writes):
        own, deps = QSEM.get(q), []
        for wr, rs in ((False, reads), (True, writes)):
            for r in rs:
                ps = SCRATCH.get(r[0], ("x",))[0] == "psum"
                for (lo, hi, w, sem, val, clk, st) in log.get(r[0], []):
                    if not ps and (hi <= r[1] or lo >= r[2]): continue
                    if not ps and st == r[3] > 2 and (lo - r[1]) % st: continue
                    if not (w or wr or ps): continue
                    if sem == own and not w: continue
                    deps.append((sem, val, clk))
        best = {}
        for sem, val, clk in deps:
            if val > best.get(sem, (0,))[0]: best[sem] = (val, clk)
        for sem, (val, clk) in sorted(best.items(), key=lambda e: -len(e[1][1])):
            if seen[q].get(sem, 0) >= val: continue
            eng[q].wait_ge(T.sem[sem], val)
            for s, v in list(clk.items()) + [(sem, val)]:
                if seen[q].get(s, 0) < v: seen[q][s] = v

    def note(accesses, w, sem, val, clk):
        for r in accesses:
            a = log.setdefault(r[0], [])
            if w and r[3] == 1: a[:] = [e for e in a if not (r[1] <= e[0] and e[1] <= r[2])]
            a.append((r[1], r[2], w, sem, val, clk, r[3]))

    def op(q, fn, writes, reads):
        need(q, reads, writes)
        count[q] += 1
        fn().then_inc(T.sem[QSEM[q]], 1)
        clk = dict(seen[q])
        clk[QSEM[q]] = count[q]
        note(reads, False, QSEM[q], count[q], clk)
        note(writes, True, QSEM[q], count[q], clk)

    def dma(sem, moves):
        for q, fn, writes, reads in moves: need(q, reads, writes)
        clk = {}
        for q, fn, writes, reads in moves:
            fn(eng[q]).then_inc(T.sem[sem], 16)
            total[sem] = total.get(sem, 0) + 16
            for s, v in seen[q].items(): clk[s] = max(v, clk.get(s, 0))
        for q, fn, writes, reads in moves:
            note(reads, False, sem, total[sem], clk)
        for q, fn, writes, reads in moves:
            note([(r[0], r[1], r[2], 2) for r in writes], True, sem, total[sem], clk)

    def arrives(sem, val, regions):
        total[sem] = val
        note(regions, True, sem, val, {})

    def send(dst, out, inn, sem, region):
        need("g", [region], [])
        rid, pid, _ = topo.addr(dst)
        es = topo.engines(core, dst)[:8]
        g.remote_dma(out, inn, T.sem[sem], T.sem["sent"], pid, rid, sum(1 << e for e in es))
        total["sent"] = total.get("sent", 0) + len(es)

    ENG = 8

    def R(name, lo=0, hi=None, st=1): return (name, lo, SCRATCH[name][1][1] if hi is None else hi, st)
    def ap(r): return T[r[0]][:, r[1]:r[2]:r[3]] if r[3] != 1 else T[r[0]][:, r[1]:r[2]]
    slots = {"lst": 0, "fs": 0, "ist": 0}
    def new(name, n=20):
        a = slots[name]
        slots[name] += n
        return R(name, a, a + n)
    def part(r, a, b): return (r[0], r[1] + a, r[1] + b, 1)

    def tt(out, a, b, o): op("v", lambda: g.vector.tensor_tensor(ap(out), ap(a), ap(b), o), [out], [a, b])
    def ts(out, a, s1, o1, s2=None, o2=None):
        if o2 is None: op("v", lambda: g.vector.tensor_scalar(ap(out), ap(a), s1, None, o1), [out], [a])
        else: op("v", lambda: g.vector.tensor_scalar(ap(out), ap(a), s1, s2, o1, o2), [out], [a])
    def cp(out, a): op("v", lambda: g.vector.tensor_copy(ap(out), ap(a)), [out], [a])
    def gv(out, win, off): op("v", lambda: g.vector.tensor_copy(ap(out), ap(win).indirect(ap(off))), [out], [win, off])
    def ga(out, win, off): op("a", lambda: g.scalar.activation(ap(out), ap(win).indirect(ap(off)), AF.Copy), [out], [win, off])
    def gt(out, win, off, b, o): op("v", lambda: g.vector.tensor_tensor(ap(out), ap(win).indirect(ap(off)), ap(b), o), [out], [win, off, b])
    def act(out, a, scale=1.0): op("a", lambda: g.scalar.activation(ap(out), ap(a), AF.Copy, scale=scale), [out], [a])
    def quant(q, s, a): op("v", lambda: g.vector.quantize_mx(ap(q), ap(s), ap(a)), [q, s], [a])
    def mm(out, l, ls, r, rs): op("t", lambda: g.tensor.matmul_mx(ap(out), ap(l), ap(ls), ap(r), ap(rs), True, True), [out], [l, ls, r, rs])
    def iota(out, pattern, base, cm, flag=False):
        op("g", lambda: g.iota(ap(out), pattern, base, cm, allow_small_or_imprecise_dtypes=True) if flag else g.iota(ap(out), pattern, base, cm), [out], [])
    turn = [0]
    def scan(n):
        m, s = R("mo%d" % turn[0], 0, n), R("so%d" % turn[0], 0, n)
        op("v", lambda: g.vector.tensor_tensor_scan(ap(s), T["rz"][:, 0:n], ap(m), 0.0, OP.mult, OP.add), [s], [m, R("rz", 0, n)])
        turn[0] ^= 1
        return (s[0], 15, n, 16)
    def pick(win, off, n=320):
        gt(R("mo%d" % turn[0], 0, n), win, off, R("mk", 0, n), OP.mult)
        return scan(n)
    def wrapped(v, n=20):
        o = new("lst", n)
        ts(o, v, 160.0, OP.add)
        return o

    dma("d_nl", [("s", lambda e: e.dma_start(T.nli[:], T.nl[:]), [R("nli")], [])])
    dma("d_u", [("a", lambda e: e.dma_start(T.ut[:], T.u[:]), [R("ut")], [])])
    for h, q in ((0, "s"), (1, "a")):
        dma("d_x%d" % h, [(q, lambda e, h=h: e.dma_start(T.xt0[:, 640 * h:640 * h + 640], T.x[:, 640 * h:640 * h + 640]), [R("xt0", 640 * h, 640 * h + 640)], [])])
    dma("d_w", [("s", lambda e: e.dma_start(T.wq[:, 0:512].bitcast(dt.uint8), T.wc[:, 0:2048]), [R("wq")], []),
                ("s", lambda e: e.dma_start(T.wsp[:, 0:512], T.ws[:, 0:512]), [R("wsp")], [])])
    dma("d_v", [("s", lambda e: e.dma_start(T.vt[:], T.v[:]), [R("vt")], [])])

    iota(R("pi"), [[0, 20]], 0, 1)
    iota(R("qi"), [[16, 20]], 0, 0)
    iota(R("ui"), [[1, 3], [16, 8]], -16, 0)
    iota(R("jmp"), [[1, 16]], 128, -1)
    iota(R("icf"), [[1, 320]], -160, 0, True)
    op("v", lambda: g.vector.memset(T.rz[:], 1.0), [R("rz")], [])
    op("v", lambda: g.vector.memset(T.rz[:, 0:320:16], 0.0), [("rz", 0, 320, 16)], [])
    ts(R("pa"), R("pi"), 15, OP.bitwise_and)
    tt(R("cw"), R("pa"), R("qi"), OP.add)
    ts(R("ccw"), R("cw"), -160.0, OP.add)
    ts(R("ua"), R("ui"), 127, OP.bitwise_and)
    cp(R("uo"), R("ua"))
    ts(R("jma"), R("jmp"), 15, OP.bitwise_and)
    ts(R("mk", 0, 16), R("jma"), 0.0, OP.is_equal)
    for a, b in ((16, 32), (32, 64), (64, 128), (128, 256), (256, 320)): cp(R("mk", a, b), R("mk", 0, b - a))
    nI = R("nli")
    nW, par = new("lst"), new("ist")
    cp(nW, nI)
    ts(par, nI, 1, OP.bitwise_and)
    def other(nI, par):
        a, b, o = new("ist"), new("ist"), new("lst")
        ts(a, par, -2.0, OP.mult, 1.0, OP.add)
        tt(b, nI, a, OP.add)
        cp(o, b)
        return o
    nxW = other(nI, par)
    NF, XF, SG = [R("nf0"), R("nf1")], [R("xf0"), R("xf1")], [R("sg0"), R("sg1")]
    ga(NF[0], R("icf"), nW)
    op("v", lambda: g.vector.tensor_copy(ap(XF[0]).indirect(ap(nxW)), ap(R("icf"))), [XF[0]], [nxW, R("icf")])
    at = [0]
    def publish(xf, nW, par):
        pub, c = "pub%d" % at[0], R("cw")
        at[0] ^= 1
        v = pick(xf, nW)
        dmc, h, t = R(pub, 0, 20), R(pub, 20, 40), new("fs")
        tt(dmc, v, R("ccw"), OP.subtract)
        tt(t, par, dmc, OP.mult)
        tt(h, t, c, OP.add)
        dma("d_sh", [("s", lambda e: e.dma_start(T.shl[16:128, :], T[pub][0:112, :]), [R("shl")], [R(pub)]),
                     ("s", lambda e: e.dma_start(T.shl[0:16, :], T[pub][112:128, :]), [R("shl")], [R(pub)])])
    publish(XF[0], nW, par)
    quant(R("qu"), R("qus"), R("ut"))
    op("v", lambda: g.vector.tensor_copy(T.uv[:, 0:384].bitcast(dt.uint32), T.qu[:, 0:128].bitcast(dt.uint32).indirect(T.uo[:, 0:24])), [R("uv")], [R("qu"), R("uo")])
    op("a", lambda: g.scalar.activation(T.uvs[:, 0:384], T.qus[:, 0:128].indirect(T.uo[:, 0:24]), AF.Copy), [R("uvs")], [R("qus"), R("uo")])

    def bank(half, b): return R("p%d" % (4 * half + b), 0, 160)
    def scores(k, half):
        c = 160 * half
        q, s = R("xq%d" % k, c, c + 160), R("xs%d" % k, c, c + 160)
        quant(q, s, R("xt%d" % k, 4 * c, 4 * c + 640))
        if k < 3:
            for j in range(3):
                mm(bank(half, j), R("uv", 128 * j, 128 * j + 128), R("uvs", 128 * j, 128 * j + 128), q, s)
    def signs(half, j):
        f = R("fw", 320 * j + 160 * half, 320 * j + 160 * half + 160)
        op("a", lambda: g.scalar.activation(ap(f), ap(bank(half, j)), AF.Sign), [f], [bank(half, j)])
        op("a", lambda: g.scalar.activation(ap(f), ap(f), AF.Relu), [f], [f])
    def flags(half, j):
        ts(R("fw", 320 * j + 160 * half, 320 * j + 160 * half + 160), bank(half, j), 0.0, OP.is_gt)
    def halves(k):
        act(R("xg"), R("xt%d" % k), 0.5)
        for b in range(4): act(R("xh", 320 * b, 320 * b + 320), (("xt%d" % k), b, 1280, 4), 0.5)

    scores(0, 0)
    scores(0, 1)
    tt(R("mo%d" % turn[0]), XF[0], R("mk"), OP.mult)
    ixW = wrapped(scan(320))
    for h in (0, 1): flags(h, 0)
    cur = [0]
    for k, s in enumerate(STEP):
        src, dst = T.cores[(rank - s) % N], T.cores[(rank + s) % N]
        rn, ri, rd = "rn%d" % k, "ri%d" % k, "rd%d" % k
        for j in range(3):
            last = j == 2
            nf, xf, sg = NF[cur[0]], XF[cur[0]], SG[cur[0]]
            cur[0] ^= 1
            nf2, xf2 = NF[cur[0]], XF[cur[0]]
            h, t, u, sW = new("lst"), new("fs"), new("fs"), new("lst")
            cp(h, R("shl", 20, 40))
            v = pick(R("fw", 320 * j, 320 * j + 320), h)
            tt(t, v, R("shl", 0, 20), OP.mult)
            tt(u, t, R("cw"), OP.add)
            cp(sW, u)
            ga(sg, R("icf"), sW)
            ga(xf2, sg, ixW)
            if j == 0:
                for hh, jj in ((0, 1), (0, 2)) if k else ((0, 1), (1, 1), (0, 2), (1, 2)): signs(hh, jj)
            v = pick(nf, sW)
            nW = wrapped(v)
            if last: send(src, T["ln%d" % k][:, 0:10], ap(part(nW, 0, 10)), rn, part(nW, 0, 10))
            if not last:
                nI, par = new("ist"), new("ist")
                ts(nI, v, 160.0, OP.add)
                ts(par, nI, 1, OP.bitwise_and)
                publish(xf2, nW, par)
                ixW = wrapped(pick(sg, ixW))
                if j == 0:
                    halves(k)
                    if k == 0:
                        op("v", lambda: g.vector.memset(T.et[:], 1.0), [R("et")], [])
                        ts(R("yt0"), R("xt0"), 32.0, OP.mult)
                        op("g", lambda: g.affine_select(T.et[:, 0:512], T.et[:, 0:512], [[1, 512]], OP.is_equal, 0.0, 0, -4), [R("et", 0, 512)], [R("et", 0, 512)])
                        for b in range(1, 4):
                            op("g", lambda b=b: g.affine_select(T.et[:, 512 * b:512 * b + 512], T.et[:, 512 * b:512 * b + 512], [[1, 512]], OP.is_equal, 0.0, -b, -4), [R("et", 512 * b, 512 * b + 512)], [R("et", 512 * b, 512 * b + 512)])
                if j == 1 and k == 0: quant(R("eq"), R("es"), R("et"))
                ga(nf2, nf, sW)
            else:
                nI, par = new("ist"), new("ist")
                ixW = wrapped(pick(sg, ixW))
                send(dst, T["li%d" % k][:, 0:20], ap(ixW), ri, ixW)
                ga(nf2, nf, sW)
                ts(nI, v, 160.0, OP.add)
        for b in range(4):
            w = R("xh", 320 * b, 320 * b + 320)
            gt(R("zn", 320 * b, 320 * b + 320), w, ixW, ("xg", b, 1280, 4), OP.add)
        arrives(rn, ENG, [R("ln%d" % k)])
        for b in range(4):
            (gv if b < 2 else ga)(("ft", b, 640, 4), R("zn", 320 * b, 320 * b + 320), R("ln%d" % k))
        fq, fp = R("fq%d" % k), R("fp%d" % k)
        quant(fq, fp, R("ft"))
        send(dst, T["lq%d" % k][:, 0:160].bitcast(dt.uint8), ap(fq).bitcast(dt.uint8), rd, fq)
        send(dst, T["lp%d" % k][:, 0:160], ap(fp), rd, fp)
        ts(par, nI, 1, OP.bitwise_and)
        nxW = other(nI, par)
        arrives(ri, ENG, [R("li%d" % k)])
        ga(R("gf"), nf2, R("li%d" % k))
        kW = wrapped(pick(R("gf"), part(nxW, 10, 20), 160), 10)
        for b in range(4):
            ga(("vo", b, 640, 4), R("zn", 320 * b, 320 * b + 320), kW)
        if k < 2: publish(xf2, nW, par)
        def layer(half, tile):
            c = 160 * half
            q, p = R("vq%d" % k, c, c + 160), R("vp%d" % k, c, c + 160)
            quant(q, p, R(tile))
            for b in range(4): mm(bank(half, b), R("wq", 128 * b, 128 * b + 128), R("wsp", 128 * b, 128 * b + 128), q, p)
            for b in range(4): tt(("yt%d" % (k + 1), 4 * c + b, 4 * c + 640, 4), bank(half, b), ("yt%d" % k, 4 * c + b, 4 * c + 640, 4), OP.add)
            ts(R("xt%d" % (k + 1), 4 * c, 4 * c + 640), R("yt%d" % (k + 1), 4 * c, 4 * c + 640), 0.03125, OP.mult)
            scores(k + 1, half)
            if k < 2:
                flags(half, 0)
            else: out(half)
        def out(half):
            c = 160 * half
            q, p = R("xq3", c, c + 160), R("xs3", c, c + 160)
            mm(bank(half, 0), R("qv"), R("qvs"), q, p)
            dma("d_os", [("s", lambda e: e.dma_start(T.oc[:, 4 * c:4 * c + 640], ap(q).bitcast(dt.uint8)), [], [q])] +
                [("s", lambda e, i=i: e.dma_start(T.osc[4 * i:4 * i + 4, c:c + 160], T.xs3[32 * i:32 * i + 4, c:c + 160]), [], [p]) for i in range(4)])
            y = R("yo", c, c + 160)
            act(y, bank(half, 0))
            dma("d_os", [("a", lambda e: e.dma_start(T.y[:, c:c + 160], ap(y)), [], [y])])
        if k == 2:
            quant(R("qv"), R("qvs"), R("vt"))
            ts(R("nmf"), nf2, 160.0, OP.add)
            dma("d_os", [("s", lambda e: e.dma_start(T.nm[:], T.nmf[0:128:16, :]), [], [R("nmf")])])
        layer(1, "vo")
        arrives(rd, 2 * ENG, [R("lq%d" % k), R("lp%d" % k)])
        for b in range(4): mm(bank(0, b), R("eq", 128 * b, 128 * b + 128), R("es", 128 * b, 128 * b + 128), R("lq%d" % k), R("lp%d" % k))
        for b in (0, 2, 1, 3): (cp if b % 2 else act)(("vf", b, 640, 4), bank(0, b))
        if k < 2:
            for jj in (1, 2): signs(1, jj)
        layer(0, "vf")
    for q, sem in QSEM.items(): total[sem] = count[q]
    for sem, val in total.items(): g.wait_ge(T.sem[sem], val)
